import numpy as np
import ml_dtypes


def mxq(x, axis, fmt="e4m3"):
    dtype, down = {"e4m3": (ml_dtypes.float8_e4m3fn, 7), "e5m2": (ml_dtypes.float8_e5m2, 14)}[fmt]
    v = np.moveaxis(np.asarray(x, np.float32).astype(ml_dtypes.bfloat16).astype(np.float64), axis, -1)
    blocks = v.reshape(v.shape[:-1] + (-1, 32))
    amax = np.abs(blocks).max(-1, keepdims=True)
    byte = np.maximum(np.where(amax > 0, np.frexp(amax)[1] - 1 + 127, 0) - down, 1)
    scale = np.exp2(byte - 127.0)
    codes = (blocks / scale).astype(np.float32).astype(dtype).astype(np.float64)
    return np.moveaxis((codes * scale).reshape(v.shape), -1, axis)


WIDE = False


def mx_kscale(k):
    if not WIDE:
        return np.ones(k)
    levels = np.array([10, -10, 5, -5, 0])
    if k % 512:
        return np.exp2(np.random.permutation(np.resize(levels, k // 32))).repeat(32)
    a = np.empty((k // 512, 16))
    for p in range(k // 512):
        a[p, :8] = np.random.permutation(np.resize(levels, 8))
        for g in range(8):
            far = levels[np.abs(levels - a[p, g]) >= 10]
            a[p, g + 8] = far[np.random.randint(len(far))]
    return np.exp2(a.ravel()).repeat(32)


def f64(x):
    return np.asarray(x).astype(np.float64)


def striped(idx):
    return np.tile(np.asarray(idx).reshape(-1, 16).T, (8, 1)).astype(np.uint16)


def unstriped(offs):
    return offs[:16].T.reshape(-1).astype(np.int64)


def striped8(idx):
    return np.asarray(idx).reshape(8, -1, 16).transpose(0, 2, 1).reshape(128, -1).astype(np.uint16)


def unstriped8(offs):
    return offs.reshape(8, 16, -1).transpose(0, 2, 1).reshape(8, -1).astype(np.int64)


def pick8(x, idx, run):
    r = np.arange(len(x))
    return x[r[:, None], idx[r % (8 * run) // run]]


E2M1 = np.array([0.0, 0.5, 1.0, 1.5, 2.0, 3.0, 4.0, 6.0, -0.0, -0.5, -1.0, -1.5, -2.0, -3.0, -4.0, -6.0])


def pack_weight(w, fmt):
    k, n = w.shape
    w = f64(np.asarray(w, np.float32).astype(ml_dtypes.bfloat16)).reshape(k // 32, 32, n)
    amax = np.abs(w).max(1)
    if fmt == "e4m3":
        byte = np.frexp(amax)[1] - 1 + 127 - 7
    else:
        mant, ex = np.frexp(amax / 6.0)
        byte = np.where(mant > 0.5, ex, ex - 1) + 127
    byte = np.clip(np.where(amax > 0, byte, 1), 1, 254)
    scaled = (w * np.exp2(127.0 - byte)[:, None, :]).reshape(k, n).astype(np.float32)
    by_word = np.ascontiguousarray(scaled.reshape(k // 512, 128, 4, n).transpose(0, 1, 3, 2))
    if fmt == "e4m3":
        words = by_word.astype(ml_dtypes.float8_e4m3fn).view(np.uint8)
    else:
        c = by_word.astype(ml_dtypes.float4_e2m1fn).view(np.uint8) & 0xF
        words = (c[..., 0::2] | (c[..., 1::2] << 4)).reshape(k // 512, 128, 2 * n)
    return np.ascontiguousarray(words), np.ascontiguousarray(byte.astype(np.uint8).reshape(k // 512, 16, n))


def unpack_weight(words, scales, fmt):
    g, _, n = scales.shape
    words = np.ascontiguousarray(words).reshape(g, 128, n, -1)
    if fmt == "e4m3":
        vals = words.view(ml_dtypes.float8_e4m3fn).astype(np.float64)
    else:
        nib = np.empty((g, 128, n, 4), np.uint8)
        nib[..., 0::2] = words & 0xF
        nib[..., 1::2] = words >> 4
        vals = E2M1[nib]
    vals = vals * np.repeat(np.exp2(scales.astype(np.float64) - 127.0), 8, axis=1)[..., None]
    return vals.transpose(0, 1, 3, 2).reshape(g * 512, n)


K, J, R, T, Z, M, C, O, N = 512, 256, 512, 512, 512, 1024, 512, 128, 256


def setup_inputs():
    n = np.random.standard_normal
    idx = np.stack([np.random.permutation(T)[:J] for _ in range(8)])
    idx2 = np.stack([np.random.permutation(T)[:J] for _ in range(8)])
    idx3 = np.random.permutation(M)[:J]
    idx4 = np.stack([np.random.permutation(C)[:J] for _ in range(8)])
    idx5 = np.random.permutation(C)[:J]
    idx6 = np.random.permutation(C)[:O]
    idx7 = np.stack([np.random.permutation(C)[:O] for _ in range(8)])
    fk = mx_kscale(K)
    fr = mx_kscale(R)
    fz = mx_kscale(Z)
    wp = pack_weight(n((K, R)) * 1 / np.sqrt(K) / fk[:, None] * fr, "e2m1")
    xop = pack_weight(n((Z, M)) / fz[:, None], "e2m1")
    w2p = pack_weight(n((Z, R)) * 1 / np.sqrt(Z) * fz[:, None] * fr, "e4m3")
    wbp = pack_weight(n((R, N)) * 1 / np.sqrt(R) / fr[:, None], "e4m3")
    return {
        "ta": (np.random.randint(-7, 8, (K, T)).astype(np.float64)).astype(np.float32),
        "ga": ((np.random.randint(10, 25, (K, 1)) / 64.0) * fk[:, None]).astype(np.float32),
        "gb": ((np.random.randint(4, 13, (K, 1)) / 64.0) * fk[:, None]).astype(np.float32),
        "w_words": wp[0],
        "w_scales": wp[1],
        "xo_words": xop[0],
        "xo_scales": xop[1],
        "w2_words": w2p[0],
        "w2_scales": w2p[1],
        "sa": (np.random.uniform(0.5, 1.6, (R, 1))).astype(np.float32),
        "sb": (np.random.uniform(0.5, 1.6, (R, 1))).astype(np.float32),
        "wb_words": wbp[0],
        "wb_scales": wbp[1],
        "offs": striped8(idx),
        "offs2": striped8(idx2),
        "offs3": striped(idx3),
        "offs4": striped8(idx4),
        "offs5": striped(idx5),
        "offs6": striped(idx6),
        "offs7": striped8(idx7),
    }


def reference(ta, ga, gb, w_words, w_scales, xo_words, xo_scales, w2_words, w2_scales, sa, sb, wb_words, wb_scales, offs, offs2, offs3, offs4, offs5, offs6, offs7):
    idx = unstriped8(offs)
    idx2 = unstriped8(offs2)
    idx3 = unstriped(offs3)
    idx4 = unstriped8(offs4)
    idx5 = unstriped(offs5)
    idx6 = unstriped(offs6)
    idx7 = unstriped8(offs7)
    wu = unpack_weight(w_words, w_scales, "e2m1")
    xou = unpack_weight(xo_words, xo_scales, "e2m1")
    w2u = unpack_weight(w2_words, w2_scales, "e4m3")
    wbu = unpack_weight(wb_words, wb_scales, "e4m3")
    xc = pick8(f64(ta), idx, 64) * f64(ga) + pick8(f64(ta), idx2, 64) * f64(gb)
    xcq = mxq(xc, 0, "e4m3")
    a = wu.T @ xcq
    xoidx3g = xou[:, idx3]
    b = w2u.T @ xoidx3g
    pw = np.zeros((R, C))
    pw[np.arange(R)[:, None], idx4[np.arange(R) % 512 // 64]] = a
    pv = np.zeros((R, C))
    pv[:, idx5] = b
    pg = pw + pv
    hid = np.maximum(pg[:, idx6] * f64(sa), pick8(pg, idx7, 64) * f64(sb))
    hidq = mxq(hid, 0, "e4m3")
    y = wbu.T @ hidq
    return y

@@ -1,0 +1,211 @@
+from contextlib import ExitStack
+
+import concourse.mybir as mybir
+
+K, J, R, T, Z, M, C, O, N = 512, 256, 512, 512, 512, 1024, 512, 128, 256
+FLOPS = 2 * K * R * J + 2 * Z * R * J + 2 * R * N * O
+
+F32 = mybir.dt.float32
+BF16 = mybir.dt.bfloat16
+I32 = mybir.dt.int32
+U32 = mybir.dt.uint32
+U16 = mybir.dt.uint16
+U8 = mybir.dt.uint8
+FP8X4 = mybir.dt.float8_e4m3fn_x4
+FP4X4 = mybir.dt.float4_e2m1fn_x4
+COPY = mybir.ActivationFunctionType.Copy
+ADD = mybir.AluOpType.add
+MAX = mybir.AluOpType.max
+
+P = 128
+PACK = 4
+
+
+def tile_picked_refined_plain_two_twoposts_one_plain_kernel(
+    tc, ta, ga, gb, w_words, w_scales, xo_words, xo_scales, w2_words, w2_scales, sa, sb, wb_words, wb_scales,
+    offs, offs2, offs3, offs4, offs5, offs6, offs7, out,
+):
+    nc = tc.nc
+    with ExitStack() as ctx:
+        keep = ctx.enter_context(tc.tile_pool(name="keep", bufs=1))
+        psum = ctx.enter_context(tc.psum_pool(name="psum", bufs=1))
+
+        def tile(name, shape, dtype, tag=None):
+            return keep.tile(shape, dtype, name=name, tag=tag or name, align_bytes=64)
+
+        def load_list(name, src):
+            dst = keep.tile(list(src.shape), U16, name=name)
+            nc.sync.dma_start(dst[:], src)
+            return dst
+
+        def load_rowwise(name, src, queue=nc.sync):
+            dst = tile(name, [P, PACK], F32)
+            queue.dma_start(dst[:], src.rearrange("(p t) one -> p (t one)", t=PACK))
+            return dst
+
+        def load_ta(t):
+            dst = tile(f"ta{t}", [P, T], F32)
+            nc.sync.dma_start(dst[:], ta.rearrange("(p t) c -> p t c", t=PACK)[:, t, :])
+            return dst
+
+        def load_bytes(name, src, cols, dtype):
+            dst = tile(name, [P, cols], dtype)
+            nc.sync.dma_start(dst[:].bitcast(I32), src.bitcast(I32))
+            return dst
+
+        def zeroed_plane(name, cols):
+            plane = tile(name, [P, cols], U8)
+            nc.vector.memset(plane[:].bitcast(I32), 0)
+            return plane
+
+        def load_plane(plane, src):
+            for q in range(4):
+                nc.sync.dma_start(plane[32 * q : 32 * q + 4, :].bitcast(I32), src[0, 4 * q : 4 * q + 4, :].bitcast(I32))
+
+        def load_staged(name, src):
+            cols = src.shape[2] // 4
+            stage = tile(name, [4, 4, cols], I32)
+            nc.sync.dma_start(stage[:], src[0].bitcast(I32).rearrange("(q r) n -> r q n", r=4))
+            return stage
+
+        def spread(plane, stage):
+            for q in range(4):
+                nc.vector.tensor_copy(out=plane[32 * q : 32 * q + 4, :].bitcast(I32), in_=stage[:, q, :])
+
+        xo_plane = zeroed_plane("xo_plane", M)
+        w2_plane = zeroed_plane("w2_plane", R)
+        w_plane = zeroed_plane("w_plane", R)
+        wb_plane = zeroed_plane("wb_plane", N)
+        pv = [tile(f"pv{t}", [P, C], F32) for t in range(2)]
+        pw = [tile(f"pw{t}", [P, C], F32) for t in range(PACK)]
+        for board in pv + pw:
+            nc.vector.memset(board[:], 0.0)
+
+        l1 = load_list("l1", offs)
+        ga_sb = load_rowwise("ga_sb", ga)
+        ta_sb = [load_ta(0)]
+        xo_stage = load_staged("xo_stage", xo_scales)
+        w2_stage = load_staged("w2_stage", w2_scales)
+        l2 = load_list("l2", offs2)
+        gb_sb = load_rowwise("gb_sb", gb, nc.gpsimd)
+        ta_sb.append(load_ta(1))
+        xo_sb = load_bytes("xo_sb", xo_words[0], M, U16)
+        l3 = load_list("l3", offs3)
+        w2_sb = load_bytes("w2_sb", w2_words[0].rearrange("p n t -> p (n t)"), R, U32)
+        ta_sb.append(load_ta(2))
+        w_sb = load_bytes("w_sb", w_words[0], 2 * R, U8)
+        ta_sb.append(load_ta(3))
+        l5 = load_list("l5", offs5)
+        load_plane(w_plane, w_scales)
+        l4 = load_list("l4", offs4)
+        l6 = load_list("l6", offs6)
+        l7 = load_list("l7", offs7)
+        sa_sb = load_rowwise("sa_sb", sa)
+        sb_sb = load_rowwise("sb_sb", sb)
+        wb_sb = load_bytes("wb_sb", wb_words[0].rearrange("p n t -> p (n t)"), N, U32)
+        load_plane(wb_plane, wb_scales)
+
+        coarse = tile("coarse", [P, PACK, J], F32)
+        fine = tile("fine", [P, PACK, J], F32)
+        for t in range(PACK):
+            nc.scalar.activation(out=coarse[:, t, :], in_=ta_sb[t][:].indirect(l1[:]), func=COPY, scale=ga_sb[:, t : t + 1])
+            nc.scalar.activation(out=fine[:, t, :], in_=ta_sb[t][:].indirect(l2[:]), func=COPY, scale=gb_sb[:, t : t + 1])
+
+        xog = tile("xog", [P, J], U16)
+        xog_plane = tile("xog_plane", [P, J], U8)
+        spread(w2_plane, w2_stage)
+        spread(xo_plane, xo_stage)
+        nc.vector.tensor_copy(out=xog[:], in_=xo_sb[:].indirect(l3[:]))
+        nc.vector.tensor_copy(out=xog_plane[:], in_=xo_plane[:].indirect(l3[:]))
+        w2_dealt = tile("w2_dealt", [P, PACK, P], U32)
+        w2_plane_dealt = tile("w2_plane_dealt", [P, PACK, P], U8)
+        nc.vector.tensor_copy(out=w2_dealt[:], in_=w2_sb[:].rearrange("p (m t) -> p t m", t=PACK))
+        nc.gpsimd.tensor_copy(out=w2_plane_dealt[:], in_=w2_plane[:].rearrange("p (m t) -> p t m", t=PACK))
+        b_sb = []
+        for pair in range(2):
+            b_ps = psum.tile([P, 2, J], F32, name=f"b_ps{pair}")
+            for u in range(2):
+                t = 2 * pair + u
+                nc.tensor.matmul_mx(
+                    out=b_ps[:, u, :], lhsT=w2_dealt[:, t, :].bitcast(FP8X4), lhsT_scale=w2_plane_dealt[:, t, :],
+                    rhs=xog[:].bitcast(FP4X4), rhs_scale=xog_plane[:], start=True, stop=True,
+                )
+            b_pair = tile(f"b_sb{pair}", [P, 2, J], F32)
+            nc.vector.tensor_copy(out=b_pair[:], in_=b_ps[:])
+            b_sb += [b_pair[:, 0, :], b_pair[:, 1, :]]
+
+        w_dealt = tile("w_dealt", [P, PACK, 2 * P], U8)
+        w_plane_dealt = tile("w_plane_dealt", [P, PACK, P], U8)
+        nc.gpsimd.tensor_copy(
+            out=w_dealt[:].rearrange("p t (m two) -> p t m two", two=2),
+            in_=w_sb[:].rearrange("p (m t two) -> p t m two", t=PACK, two=2),
+        )
+        nc.gpsimd.tensor_copy(out=w_plane_dealt[:], in_=w_plane[:].rearrange("p (m t) -> p t m", t=PACK))
+
+        xc = tile("xc", [P, J * PACK], BF16)
+        nc.vector.tensor_tensor(
+            out=xc[:].rearrange("p (c i t) -> p c t i", i=4, t=PACK),
+            in0=coarse[:].rearrange("p t (c i) -> p c t i", i=4),
+            in1=fine[:].rearrange("p t (c i) -> p c t i", i=4),
+            op=ADD,
+        )
+        xc_codes = tile("xc_codes", [P, J], U32)
+        xc_plane = tile("xc_plane", [P, J], U8)
+        nc.vector.quantize_mx(out=xc_codes[:].bitcast(FP8X4), scales=xc_plane[:], in_=xc[:])
+
+        a_ps = []
+        for t in range(PACK):
+            a_ps.append(psum.tile([P, J], F32, name=f"a_ps{t}"))
+            nc.tensor.matmul_mx(
+                out=a_ps[t][:], lhsT=w_dealt[:, t, :].bitcast(FP4X4), lhsT_scale=w_plane_dealt[:, t, :],
+                rhs=xc_codes[:].bitcast(FP8X4), rhs_scale=xc_plane[:], start=True, stop=True,
+            )
+        for t, tag in ((2, "w_dealt"), (3, "xc_codes")):
+            pv.append(tile(f"pv{t}", [P, C], F32, tag=tag))
+            nc.gpsimd.memset(pv[t][:], 0.0)
+        a_sb = [tile(f"a_sb{t}", [P, J], F32) for t in range(PACK)]
+        pg = [tile(f"pg{t}", [P, C], F32) for t in range(PACK)]
+        first = tile("first", [P, PACK, O], F32)
+        second = tile("second", [P, PACK, O], F32)
+
+        def scatter_b(t):
+            nc.scalar.activation(out=pv[t][:].indirect(l5[:]), in_=b_sb[t], func=COPY)
+
+        def read_board(t):
+            nc.scalar.activation(out=first[:, t, :], in_=pg[t][:].indirect(l6[:]), func=COPY, scale=sa_sb[:, t : t + 1])
+            nc.scalar.activation(out=second[:, t, :], in_=pg[t][:].indirect(l7[:]), func=COPY, scale=sb_sb[:, t : t + 1])
+
+        nc.vector.tensor_copy(out=a_sb[0][:], in_=a_ps[0][:])
+        scatter_b(0)
+        scatter_b(1)
+        for t in range(1, PACK):
+            nc.scalar.copy(out=a_sb[t][:], in_=a_ps[t][:])
+        scatter_b(2)
+        scatter_b(3)
+        for t in range(PACK):
+            nc.vector.tensor_copy(out=pw[t][:].indirect(l4[:]), in_=a_sb[t][:])
+            split = 8 if t == PACK - 1 else C
+            nc.gpsimd.tensor_tensor(out=pg[t][:, :split], in0=pw[t][:, :split], in1=pv[t][:, :split], op=ADD)
+            if split < C:
+                nc.vector.tensor_tensor(out=pg[t][:, split:], in0=pw[t][:, split:], in1=pv[t][:, split:], op=ADD)
+            read_board(t)
+
+        hid = tile("hid", [P, O * PACK], BF16)
+        nc.vector.tensor_tensor(
+            out=hid[:].rearrange("p (c i t) -> p c t i", i=4, t=PACK),
+            in0=first[:].rearrange("p t (c i) -> p c t i", i=4),
+            in1=second[:].rearrange("p t (c i) -> p c t i", i=4),
+            op=MAX,
+        )
+        hid_codes = tile("hid_codes", [P, O], U32)
+        hid_plane = tile("hid_plane", [P, O], U8)
+        nc.vector.quantize_mx(out=hid_codes[:].bitcast(FP8X4), scales=hid_plane[:], in_=hid[:])
+        y_ps = psum.tile([P, 2, O], F32, name="y_ps")
+        for m in range(2):
+            nc.tensor.matmul_mx(
+                out=y_ps[:, m, :], lhsT=wb_sb[:, m * P : (m + 1) * P].bitcast(FP8X4), lhsT_scale=wb_plane[:, m * P : (m + 1) * P],
+                rhs=hid_codes[:].bitcast(FP8X4), rhs_scale=hid_plane[:], start=True, stop=True,
+            )
+        y_sb = tile("y_sb", [P, 2, O], F32)
+        nc.vector.tensor_copy(out=y_sb[:], in_=y_ps[:])
+        nc.sync.dma_start(out.rearrange("(m p) o -> p m o", p=P), y_sb[:])

@@ -62,42 +62,40 @@ def tile_picked_refined_plain_two_twoposts_one_plain_kernel(
             for q in range(4):
                 nc.sync.dma_start(plane[32 * q : 32 * q + 4, :].bitcast(I32), src[0, 4 * q : 4 * q + 4, :].bitcast(I32))
 
-        def load_staged(name, src):
-            cols = src.shape[2] // 4
-            stage = tile(name, [4, 4, cols], I32)
-            nc.sync.dma_start(stage[:], src[0].bitcast(I32).rearrange("(q r) n -> r q n", r=4))
-            return stage
+        def load_staged(stage, src):
+            nc.sync.dma_start(stage, src[0].bitcast(I32).rearrange("(q r) n -> r q n", r=4))
 
         def spread(plane, stage):
             for q in range(4):
                 nc.vector.tensor_copy(out=plane[32 * q : 32 * q + 4, :].bitcast(I32), in_=stage[:, q, :])
 
+        ww_plane = zeroed_plane("ww_plane", 2 * R)
         xo_plane = zeroed_plane("xo_plane", M)
-        w2_plane = zeroed_plane("w2_plane", R)
-        w_plane = zeroed_plane("w_plane", R)
         wb_plane = zeroed_plane("wb_plane", N)
-        pv = [tile(f"pv{t}", [P, C], F32) for t in range(2)]
-        pw = [tile(f"pw{t}", [P, C], F32) for t in range(PACK)]
+        pv = [tile(f"pv{t}", [P, C], F32) for t in range(PACK)]
+        pw = [tile(f"pw{t}", [P, C], F32) for t in range(2)]
         for board in pv + pw:
             nc.vector.memset(board[:], 0.0)
 
+        ww_stage = tile("ww_stage", [4, 4, 2 * R // 4], I32)
+        xo_stage = tile("xo_stage", [4, 4, M // 4], I32)
         l1 = load_list("l1", offs)
         ga_sb = load_rowwise("ga_sb", ga)
         ta_sb = [load_ta(0)]
-        xo_stage = load_staged("xo_stage", xo_scales)
-        w2_stage = load_staged("w2_stage", w2_scales)
-        l2 = load_list("l2", offs2)
+        load_staged(ww_stage[:, :, : R // 4], w2_scales)
+        load_staged(ww_stage[:, :, R // 4 :], w_scales)
+        load_staged(xo_stage[:], xo_scales)
         gb_sb = load_rowwise("gb_sb", gb, nc.gpsimd)
         ta_sb.append(load_ta(1))
         xo_sb = load_bytes("xo_sb", xo_words[0], M, U16)
+        l2 = load_list("l2", offs2)
         l3 = load_list("l3", offs3)
         w2_sb = load_bytes("w2_sb", w2_words[0].rearrange("p n t -> p (n t)"), R, U32)
         ta_sb.append(load_ta(2))
         w_sb = load_bytes("w_sb", w_words[0], 2 * R, U8)
         ta_sb.append(load_ta(3))
-        l5 = load_list("l5", offs5)
-        load_plane(w_plane, w_scales)
         l4 = load_list("l4", offs4)
+        l5 = load_list("l5", offs5)
         l6 = load_list("l6", offs6)
         l7 = load_list("l7", offs7)
         sa_sb = load_rowwise("sa_sb", sa)
@@ -105,90 +103,100 @@ def tile_picked_refined_plain_two_twoposts_one_plain_kernel(
         wb_sb = load_bytes("wb_sb", wb_words[0].rearrange("p n t -> p (n t)"), N, U32)
         load_plane(wb_plane, wb_scales)
 
+        H = J // 2
         coarse = tile("coarse", [P, PACK, J], F32)
         fine = tile("fine", [P, PACK, J], F32)
-        for t in range(PACK):
-            nc.scalar.activation(out=coarse[:, t, :], in_=ta_sb[t][:].indirect(l1[:]), func=COPY, scale=ga_sb[:, t : t + 1])
-            nc.scalar.activation(out=fine[:, t, :], in_=ta_sb[t][:].indirect(l2[:]), func=COPY, scale=gb_sb[:, t : t + 1])
 
+        def fetch_codes(t, j0, j1):
+            cols = slice(j0 // 16, j1 // 16)
+            nc.scalar.activation(out=coarse[:, t, j0:j1], in_=ta_sb[t][:].indirect(l1[:, cols]), func=COPY, scale=ga_sb[:, t : t + 1])
+            nc.scalar.activation(out=fine[:, t, j0:j1], in_=ta_sb[t][:].indirect(l2[:, cols]), func=COPY, scale=gb_sb[:, t : t + 1])
+
+        for t in range(PACK - 1):
+            fetch_codes(t, 0, J)
+        fetch_codes(PACK - 1, 0, H)
+        fetch_codes(PACK - 1, H, J)
+
+        spread(ww_plane, ww_stage)
+        spread(xo_plane, xo_stage)
+        ww_plane_dealt = tile("ww_plane_dealt", [P, 2, PACK, P], U8)
+        nc.vector.tensor_copy(out=ww_plane_dealt[:], in_=ww_plane[:].rearrange("p (w m t) -> p w t m", w=2, t=PACK))
         xog = tile("xog", [P, J], U16)
         xog_plane = tile("xog_plane", [P, J], U8)
-        spread(w2_plane, w2_stage)
-        spread(xo_plane, xo_stage)
         nc.vector.tensor_copy(out=xog[:], in_=xo_sb[:].indirect(l3[:]))
         nc.vector.tensor_copy(out=xog_plane[:], in_=xo_plane[:].indirect(l3[:]))
         w2_dealt = tile("w2_dealt", [P, PACK, P], U32)
-        w2_plane_dealt = tile("w2_plane_dealt", [P, PACK, P], U8)
-        nc.vector.tensor_copy(out=w2_dealt[:], in_=w2_sb[:].rearrange("p (m t) -> p t m", t=PACK))
-        nc.gpsimd.tensor_copy(out=w2_plane_dealt[:], in_=w2_plane[:].rearrange("p (m t) -> p t m", t=PACK))
-        b_sb = []
-        for pair in range(2):
-            b_ps = psum.tile([P, 2, J], F32, name=f"b_ps{pair}")
-            for u in range(2):
-                t = 2 * pair + u
-                nc.tensor.matmul_mx(
-                    out=b_ps[:, u, :], lhsT=w2_dealt[:, t, :].bitcast(FP8X4), lhsT_scale=w2_plane_dealt[:, t, :],
-                    rhs=xog[:].bitcast(FP4X4), rhs_scale=xog_plane[:], start=True, stop=True,
-                )
-            b_pair = tile(f"b_sb{pair}", [P, 2, J], F32)
-            nc.vector.tensor_copy(out=b_pair[:], in_=b_ps[:])
-            b_sb += [b_pair[:, 0, :], b_pair[:, 1, :]]
-
+        nc.vector.tensor_copy(
+            out=w2_dealt[:].rearrange("p t (c i) -> p c t i", i=4),
+            in_=w2_sb[:].rearrange("p (c i t) -> p c t i", i=4, t=PACK),
+        )
         w_dealt = tile("w_dealt", [P, PACK, 2 * P], U8)
-        w_plane_dealt = tile("w_plane_dealt", [P, PACK, P], U8)
-        nc.gpsimd.tensor_copy(
+        nc.vector.tensor_copy(
             out=w_dealt[:].rearrange("p t (m two) -> p t m two", two=2),
             in_=w_sb[:].rearrange("p (m t two) -> p t m two", t=PACK, two=2),
         )
-        nc.gpsimd.tensor_copy(out=w_plane_dealt[:], in_=w_plane[:].rearrange("p (m t) -> p t m", t=PACK))
+
+        def product_b(t, out_ps):
+            nc.tensor.matmul_mx(
+                out=out_ps, lhsT=w2_dealt[:, t, :].bitcast(FP8X4), lhsT_scale=ww_plane_dealt[:, 0, t, :],
+                rhs=xog[:].bitcast(FP4X4), rhs_scale=xog_plane[:], start=True, stop=True,
+            )
+
+        def scatter_b(t, b_sb):
+            nc.scalar.activation(out=pv[t][:].indirect(l5[:]), in_=b_sb, func=COPY)
+
+        b0_ps = psum.tile([P, J], F32, name="b0_ps")
+        b0_sb = tile("b0_sb", [P, J], F32)
+        product_b(0, b0_ps[:])
+        nc.vector.tensor_copy(out=b0_sb[:], in_=b0_ps[:])
+        scatter_b(0, b0_sb[:])
 
         xc = tile("xc", [P, J * PACK], BF16)
-        nc.vector.tensor_tensor(
-            out=xc[:].rearrange("p (c i t) -> p c t i", i=4, t=PACK),
-            in0=coarse[:].rearrange("p t (c i) -> p c t i", i=4),
-            in1=fine[:].rearrange("p t (c i) -> p c t i", i=4),
-            op=ADD,
-        )
         xc_codes = tile("xc_codes", [P, J], U32)
         xc_plane = tile("xc_plane", [P, J], U8)
-        nc.vector.quantize_mx(out=xc_codes[:].bitcast(FP8X4), scales=xc_plane[:], in_=xc[:])
-
-        a_ps = []
-        for t in range(PACK):
-            a_ps.append(psum.tile([P, J], F32, name=f"a_ps{t}"))
-            nc.tensor.matmul_mx(
-                out=a_ps[t][:], lhsT=w_dealt[:, t, :].bitcast(FP4X4), lhsT_scale=w_plane_dealt[:, t, :],
-                rhs=xc_codes[:].bitcast(FP8X4), rhs_scale=xc_plane[:], start=True, stop=True,
+        for j0 in (0, H):
+            xc_half = xc[:, j0 * PACK : (j0 + H) * PACK]
+            nc.vector.tensor_tensor(
+                out=xc_half.rearrange("p (c i t) -> p c t i", i=4, t=PACK),
+                in0=coarse[:, :, j0 : j0 + H].rearrange("p t (c i) -> p c t i", i=4),
+                in1=fine[:, :, j0 : j0 + H].rearrange("p t (c i) -> p c t i", i=4),
+                op=ADD,
             )
-        for t, tag in ((2, "w_dealt"), (3, "xc_codes")):
-            pv.append(tile(f"pv{t}", [P, C], F32, tag=tag))
-            nc.gpsimd.memset(pv[t][:], 0.0)
-        a_sb = [tile(f"a_sb{t}", [P, J], F32) for t in range(PACK)]
+            nc.vector.quantize_mx(out=xc_codes[:, j0 : j0 + H].bitcast(FP8X4), scales=xc_plane[:, j0 : j0 + H], in_=xc_half)
+        for t, tag in ((2, "fine"), (3, "xc")):
+            pw.append(tile(f"pw{t}", [P, C], F32, tag=tag))
+            nc.vector.memset(pw[t][:], 0.0)
+
+        def product_a(t, j0, j1, out_ps):
+            nc.tensor.matmul_mx(
+                out=out_ps, lhsT=w_dealt[:, t, :].bitcast(FP4X4), lhsT_scale=ww_plane_dealt[:, 1, t, :],
+                rhs=xc_codes[:, j0:j1].bitcast(FP8X4), rhs_scale=xc_plane[:, j0:j1], start=True, stop=True,
+            )
+
+        a0_sb = tile("a0_sb", [P, J], F32)
+        for j0 in (0, H):
+            a0_ps = psum.tile([P, H], F32, name=f"a0_ps{j0}")
+            product_a(0, j0, j0 + H, a0_ps[:])
+            nc.scalar.copy(out=a0_sb[:, j0 : j0 + H], in_=a0_ps[:])
+        a_sb = [a0_sb[:]]
+        for t in range(1, PACK):
+            ab_ps = psum.tile([P, 2, J], F32, name=f"ab_ps{t}", tag="ab_ps")
+            ab_sb = tile(f"ab_sb{t}", [P, 2, J], F32)
+            product_b(t, ab_ps[:, 1, :])
+            product_a(t, 0, J, ab_ps[:, 0, :])
+            nc.scalar.copy(out=ab_sb[:], in_=ab_ps[:])
+            scatter_b(t, ab_sb[:, 1, :])
+            a_sb.append(ab_sb[:, 0, :])
+
         pg = [tile(f"pg{t}", [P, C], F32) for t in range(PACK)]
         first = tile("first", [P, PACK, O], F32)
         second = tile("second", [P, PACK, O], F32)
-
-        def scatter_b(t):
-            nc.scalar.activation(out=pv[t][:].indirect(l5[:]), in_=b_sb[t], func=COPY)
-
-        def read_board(t):
+        for t in range(PACK):
+            for j0, j1 in ((0, H), (H, J)) if t == 0 else ((0, J),):
+                nc.vector.tensor_copy(out=pw[t][:].indirect(l4[:, j0 // 16 : j1 // 16]), in_=a_sb[t][:, j0:j1])
+            nc.vector.tensor_tensor(out=pg[t][:], in0=pw[t][:], in1=pv[t][:], op=ADD)
             nc.scalar.activation(out=first[:, t, :], in_=pg[t][:].indirect(l6[:]), func=COPY, scale=sa_sb[:, t : t + 1])
             nc.scalar.activation(out=second[:, t, :], in_=pg[t][:].indirect(l7[:]), func=COPY, scale=sb_sb[:, t : t + 1])
-
-        nc.vector.tensor_copy(out=a_sb[0][:], in_=a_ps[0][:])
-        scatter_b(0)
-        scatter_b(1)
-        for t in range(1, PACK):
-            nc.scalar.copy(out=a_sb[t][:], in_=a_ps[t][:])
-        scatter_b(2)
-        scatter_b(3)
-        for t in range(PACK):
-            nc.vector.tensor_copy(out=pw[t][:].indirect(l4[:]), in_=a_sb[t][:])
-            split = 8 if t == PACK - 1 else C
-            nc.gpsimd.tensor_tensor(out=pg[t][:, :split], in0=pw[t][:, :split], in1=pv[t][:, :split], op=ADD)
-            if split < C:
-                nc.vector.tensor_tensor(out=pg[t][:, split:], in0=pw[t][:, split:], in1=pv[t][:, split:], op=ADD)
-            read_board(t)
 
         hid = tile("hid", [P, O * PACK], BF16)
         nc.vector.tensor_tensor(

@@ -69,33 +69,39 @@ def tile_picked_refined_plain_two_twoposts_one_plain_kernel(
             for q in range(4):
                 nc.vector.tensor_copy(out=plane[32 * q : 32 * q + 4, :].bitcast(I32), in_=stage[:, q, :])
 
-        ww_plane = zeroed_plane("ww_plane", 2 * R)
+        warm_in = tile("warm_in", [P, 1], F32)
+        warm_out = tile("warm_out", [P, 1], F32)
+        nc.gpsimd.memset(warm_in[:], 0.0)
+        nc.scalar.activation(out=warm_out[:], in_=warm_in[:], func=COPY)
+
+        w2_plane = zeroed_plane("w2_plane", R)
         xo_plane = zeroed_plane("xo_plane", M)
+        w_plane = zeroed_plane("w_plane", R)
         wb_plane = zeroed_plane("wb_plane", N)
-        pv = [tile(f"pv{t}", [P, C], F32) for t in range(PACK)]
+        pv = [tile(f"pv{t}", [P, C], F32) for t in range(3)]
         pw = [tile(f"pw{t}", [P, C], F32) for t in range(2)]
         for board in pv + pw:
             nc.vector.memset(board[:], 0.0)
 
-        ww_stage = tile("ww_stage", [4, 4, 2 * R // 4], I32)
+        w2_stage = tile("w2_stage", [4, 4, R // 4], I32)
         xo_stage = tile("xo_stage", [4, 4, M // 4], I32)
+        ta_sb = [load_ta(0)]
         l1 = load_list("l1", offs)
         ga_sb = load_rowwise("ga_sb", ga)
-        ta_sb = [load_ta(0)]
-        load_staged(ww_stage[:, :, : R // 4], w2_scales)
-        load_staged(ww_stage[:, :, R // 4 :], w_scales)
+        load_staged(w2_stage[:], w2_scales)
         load_staged(xo_stage[:], xo_scales)
-        gb_sb = load_rowwise("gb_sb", gb, nc.gpsimd)
         ta_sb.append(load_ta(1))
         xo_sb = load_bytes("xo_sb", xo_words[0], M, U16)
-        l2 = load_list("l2", offs2)
         l3 = load_list("l3", offs3)
+        l2 = load_list("l2", offs2)
+        gb_sb = load_rowwise("gb_sb", gb)
         w2_sb = load_bytes("w2_sb", w2_words[0].rearrange("p n t -> p (n t)"), R, U32)
         ta_sb.append(load_ta(2))
+        l5 = load_list("l5", offs5)
         w_sb = load_bytes("w_sb", w_words[0], 2 * R, U8)
         ta_sb.append(load_ta(3))
+        load_plane(w_plane, w_scales)
         l4 = load_list("l4", offs4)
-        l5 = load_list("l5", offs5)
         l6 = load_list("l6", offs6)
         l7 = load_list("l7", offs7)
         sa_sb = load_rowwise("sa_sb", sa)
@@ -117,10 +123,10 @@ def tile_picked_refined_plain_two_twoposts_one_plain_kernel(
         fetch_codes(PACK - 1, 0, H)
         fetch_codes(PACK - 1, H, J)
 
-        spread(ww_plane, ww_stage)
+        spread(w2_plane, w2_stage)
         spread(xo_plane, xo_stage)
-        ww_plane_dealt = tile("ww_plane_dealt", [P, 2, PACK, P], U8)
-        nc.vector.tensor_copy(out=ww_plane_dealt[:], in_=ww_plane[:].rearrange("p (w m t) -> p w t m", w=2, t=PACK))
+        w2_plane_dealt = tile("w2_plane_dealt", [P, PACK, P], U8)
+        nc.gpsimd.tensor_copy(out=w2_plane_dealt[:], in_=w2_plane[:].rearrange("p (m t) -> p t m", t=PACK))
         xog = tile("xog", [P, J], U16)
         xog_plane = tile("xog_plane", [P, J], U8)
         nc.vector.tensor_copy(out=xog[:], in_=xo_sb[:].indirect(l3[:]))
@@ -131,56 +137,71 @@ def tile_picked_refined_plain_two_twoposts_one_plain_kernel(
             in_=w2_sb[:].rearrange("p (c i t) -> p c t i", i=4, t=PACK),
         )
         w_dealt = tile("w_dealt", [P, PACK, 2 * P], U8)
-        nc.vector.tensor_copy(
+        w_plane_dealt = tile("w_plane_dealt", [P, PACK, P], U8)
+        nc.gpsimd.tensor_copy(
             out=w_dealt[:].rearrange("p t (m two) -> p t m two", two=2),
             in_=w_sb[:].rearrange("p (m t two) -> p t m two", t=PACK, two=2),
         )
+        nc.gpsimd.tensor_copy(out=w_plane_dealt[:], in_=w_plane[:].rearrange("p (m t) -> p t m", t=PACK))
 
         def product_b(t, out_ps):
             nc.tensor.matmul_mx(
-                out=out_ps, lhsT=w2_dealt[:, t, :].bitcast(FP8X4), lhsT_scale=ww_plane_dealt[:, 0, t, :],
+                out=out_ps, lhsT=w2_dealt[:, t, :].bitcast(FP8X4), lhsT_scale=w2_plane_dealt[:, t, :],
                 rhs=xog[:].bitcast(FP4X4), rhs_scale=xog_plane[:], start=True, stop=True,
             )
 
         def scatter_b(t, b_sb):
             nc.scalar.activation(out=pv[t][:].indirect(l5[:]), in_=b_sb, func=COPY)
 
+        def interleave_pair(dst, t0, in0, in1, op):
+            nc.vector.tensor_tensor(
+                out=dst.rearrange("p (c t) -> p c t", t=PACK)[:, :, t0 : t0 + 2],
+                in0=in0[:, t0 : t0 + 2, :].rearrange("p t c -> p c t"),
+                in1=in1[:, t0 : t0 + 2, :].rearrange("p t c -> p c t"),
+                op=op,
+            )
+
         b0_ps = psum.tile([P, J], F32, name="b0_ps")
         b0_sb = tile("b0_sb", [P, J], F32)
         product_b(0, b0_ps[:])
         nc.vector.tensor_copy(out=b0_sb[:], in_=b0_ps[:])
-        scatter_b(0, b0_sb[:])
+        nc.vector.tensor_copy(out=pv[0][:].indirect(l5[:]), in_=b0_sb[:])
+        b1_ps = psum.tile([P, J], F32, name="b1_ps")
+        b1_sb = tile("b1_sb", [P, J], F32, tag="ta3")
+        product_b(1, b1_ps[:])
+        nc.scalar.copy(out=b1_sb[:], in_=b1_ps[:])
+        scatter_b(1, b1_sb[:])
 
         xc = tile("xc", [P, J * PACK], BF16)
         xc_codes = tile("xc_codes", [P, J], U32)
         xc_plane = tile("xc_plane", [P, J], U8)
+        interleave_pair(xc[:], 0, coarse[:], fine[:], ADD)
         for j0 in (0, H):
             xc_half = xc[:, j0 * PACK : (j0 + H) * PACK]
-            nc.vector.tensor_tensor(
-                out=xc_half.rearrange("p (c i t) -> p c t i", i=4, t=PACK),
-                in0=coarse[:, :, j0 : j0 + H].rearrange("p t (c i) -> p c t i", i=4),
-                in1=fine[:, :, j0 : j0 + H].rearrange("p t (c i) -> p c t i", i=4),
-                op=ADD,
-            )
+            interleave_pair(xc_half, 2, coarse[:, :, j0 : j0 + H], fine[:, :, j0 : j0 + H], ADD)
             nc.vector.quantize_mx(out=xc_codes[:, j0 : j0 + H].bitcast(FP8X4), scales=xc_plane[:, j0 : j0 + H], in_=xc_half)
-        for t, tag in ((2, "fine"), (3, "xc")):
-            pw.append(tile(f"pw{t}", [P, C], F32, tag=tag))
-            nc.vector.memset(pw[t][:], 0.0)
+        for boards, name, tag in ((pw, "pw2", "xo_sb"), (pv, "pv3", "w_plane"), (pw, "pw3", "w_plane_dealt")):
+            boards.append(tile(name, [P, C], F32, tag=tag))
+            nc.gpsimd.memset(boards[-1][:], 0.0)
 
         def product_a(t, j0, j1, out_ps):
             nc.tensor.matmul_mx(
-                out=out_ps, lhsT=w_dealt[:, t, :].bitcast(FP4X4), lhsT_scale=ww_plane_dealt[:, 1, t, :],
+                out=out_ps, lhsT=w_dealt[:, t, :].bitcast(FP4X4), lhsT_scale=w_plane_dealt[:, t, :],
                 rhs=xc_codes[:, j0:j1].bitcast(FP8X4), rhs_scale=xc_plane[:, j0:j1], start=True, stop=True,
             )
 
         a0_sb = tile("a0_sb", [P, J], F32)
-        for j0 in (0, H):
+        for j0, copy_out in ((0, nc.vector.tensor_copy), (H, nc.scalar.copy)):
             a0_ps = psum.tile([P, H], F32, name=f"a0_ps{j0}")
             product_a(0, j0, j0 + H, a0_ps[:])
-            nc.scalar.copy(out=a0_sb[:, j0 : j0 + H], in_=a0_ps[:])
-        a_sb = [a0_sb[:]]
-        for t in range(1, PACK):
-            ab_ps = psum.tile([P, 2, J], F32, name=f"ab_ps{t}", tag="ab_ps")
+            copy_out(out=a0_sb[:, j0 : j0 + H], in_=a0_ps[:])
+        a1_ps = psum.tile([P, J], F32, name="a1_ps")
+        a1_sb = tile("a1_sb", [P, J], F32)
+        product_a(1, 0, J, a1_ps[:])
+        nc.scalar.copy(out=a1_sb[:], in_=a1_ps[:])
+        a_sb = [a0_sb[:], a1_sb[:]]
+        for t in range(2, PACK):
+            ab_ps = psum.tile([P, 2, J], F32, name=f"ab_ps{t}")
             ab_sb = tile(f"ab_sb{t}", [P, 2, J], F32)
             product_b(t, ab_ps[:, 1, :])
             product_a(t, 0, J, ab_ps[:, 0, :])
@@ -194,26 +215,25 @@ def tile_picked_refined_plain_two_twoposts_one_plain_kernel(
         for t in range(PACK):
             for j0, j1 in ((0, H), (H, J)) if t == 0 else ((0, J),):
                 nc.vector.tensor_copy(out=pw[t][:].indirect(l4[:, j0 // 16 : j1 // 16]), in_=a_sb[t][:, j0:j1])
-            nc.vector.tensor_tensor(out=pg[t][:], in0=pw[t][:], in1=pv[t][:], op=ADD)
+            split = 8 if t == PACK - 1 else C
+            nc.gpsimd.tensor_tensor(out=pg[t][:, :split], in0=pw[t][:, :split], in1=pv[t][:, :split], op=ADD)
+            if split < C:
+                nc.vector.tensor_tensor(out=pg[t][:, split:], in0=pw[t][:, split:], in1=pv[t][:, split:], op=ADD)
             nc.scalar.activation(out=first[:, t, :], in_=pg[t][:].indirect(l6[:]), func=COPY, scale=sa_sb[:, t : t + 1])
             nc.scalar.activation(out=second[:, t, :], in_=pg[t][:].indirect(l7[:]), func=COPY, scale=sb_sb[:, t : t + 1])
 
         hid = tile("hid", [P, O * PACK], BF16)
-        nc.vector.tensor_tensor(
-            out=hid[:].rearrange("p (c i t) -> p c t i", i=4, t=PACK),
-            in0=first[:].rearrange("p t (c i) -> p c t i", i=4),
-            in1=second[:].rearrange("p t (c i) -> p c t i", i=4),
-            op=MAX,
-        )
+        for t0 in (0, 2):
+            interleave_pair(hid[:], t0, first[:], second[:], MAX)
         hid_codes = tile("hid_codes", [P, O], U32)
         hid_plane = tile("hid_plane", [P, O], U8)
         nc.vector.quantize_mx(out=hid_codes[:].bitcast(FP8X4), scales=hid_plane[:], in_=hid[:])
-        y_ps = psum.tile([P, 2, O], F32, name="y_ps")
-        for m in range(2):
+        for m, (bank, copy_out, queue) in enumerate((("b0_ps", nc.scalar.copy, nc.scalar), ("b1_ps", nc.vector.tensor_copy, nc.sync))):
+            y_ps = psum.tile([P, O], F32, name=f"y_ps{m}", tag=bank)
+            y_sb = tile(f"y_sb{m}", [P, O], F32)
             nc.tensor.matmul_mx(
-                out=y_ps[:, m, :], lhsT=wb_sb[:, m * P : (m + 1) * P].bitcast(FP8X4), lhsT_scale=wb_plane[:, m * P : (m + 1) * P],
+                out=y_ps[:], lhsT=wb_sb[:, m * P : (m + 1) * P].bitcast(FP8X4), lhsT_scale=wb_plane[:, m * P : (m + 1) * P],
                 rhs=hid_codes[:].bitcast(FP8X4), rhs_scale=hid_plane[:], start=True, stop=True,
             )
-        y_sb = tile("y_sb", [P, 2, O], F32)
-        nc.vector.tensor_copy(out=y_sb[:], in_=y_ps[:])
-        nc.sync.dma_start(out.rearrange("(m p) o -> p m o", p=P), y_sb[:])
+            copy_out(out=y_sb[:], in_=y_ps[:])
+            queue.dma_start(out[m * P : (m + 1) * P, :], y_sb[:])

@@ -74,32 +74,31 @@ def tile_picked_refined_plain_two_twoposts_one_plain_kernel(
         nc.gpsimd.memset(warm_in[:], 0.0)
         nc.scalar.activation(out=warm_out[:], in_=warm_in[:], func=COPY)
 
-        w2_plane = zeroed_plane("w2_plane", R)
         xo_plane = zeroed_plane("xo_plane", M)
+        w2_plane = zeroed_plane("w2_plane", R)
         w_plane = zeroed_plane("w_plane", R)
         wb_plane = zeroed_plane("wb_plane", N)
-        pv = [tile(f"pv{t}", [P, C], F32) for t in range(3)]
-        pw = [tile(f"pw{t}", [P, C], F32) for t in range(2)]
+        pv = [tile(f"pv{t}", [P, C], F32) for t in range(2)]
+        pw = [tile(f"pw{t}", [P, C], F32) for t in range(PACK)]
         for board in pv + pw:
             nc.vector.memset(board[:], 0.0)
 
-        w2_stage = tile("w2_stage", [4, 4, R // 4], I32)
         xo_stage = tile("xo_stage", [4, 4, M // 4], I32)
         ta_sb = [load_ta(0)]
         l1 = load_list("l1", offs)
         ga_sb = load_rowwise("ga_sb", ga)
-        load_staged(w2_stage[:], w2_scales)
         load_staged(xo_stage[:], xo_scales)
         ta_sb.append(load_ta(1))
         xo_sb = load_bytes("xo_sb", xo_words[0], M, U16)
         l3 = load_list("l3", offs3)
         l2 = load_list("l2", offs2)
         gb_sb = load_rowwise("gb_sb", gb)
-        w2_sb = load_bytes("w2_sb", w2_words[0].rearrange("p n t -> p (n t)"), R, U32)
         ta_sb.append(load_ta(2))
-        l5 = load_list("l5", offs5)
-        w_sb = load_bytes("w_sb", w_words[0], 2 * R, U8)
+        w2_sb = load_bytes("w2_sb", w2_words[0].rearrange("p n t -> p (n t)"), R, U32)
+        load_plane(w2_plane, w2_scales)
         ta_sb.append(load_ta(3))
+        w_sb = load_bytes("w_sb", w_words[0], 2 * R, U8)
+        l5 = load_list("l5", offs5)
         load_plane(w_plane, w_scales)
         l4 = load_list("l4", offs4)
         l6 = load_list("l6", offs6)
@@ -123,10 +122,9 @@ def tile_picked_refined_plain_two_twoposts_one_plain_kernel(
         fetch_codes(PACK - 1, 0, H)
         fetch_codes(PACK - 1, H, J)
 
-        spread(w2_plane, w2_stage)
         spread(xo_plane, xo_stage)
         w2_plane_dealt = tile("w2_plane_dealt", [P, PACK, P], U8)
-        nc.gpsimd.tensor_copy(out=w2_plane_dealt[:], in_=w2_plane[:].rearrange("p (m t) -> p t m", t=PACK))
+        nc.vector.tensor_copy(out=w2_plane_dealt[:], in_=w2_plane[:].rearrange("p (m t) -> p t m", t=PACK))
         xog = tile("xog", [P, J], U16)
         xog_plane = tile("xog_plane", [P, J], U8)
         nc.vector.tensor_copy(out=xog[:], in_=xo_sb[:].indirect(l3[:]))
@@ -153,36 +151,32 @@ def tile_picked_refined_plain_two_twoposts_one_plain_kernel(
         def scatter_b(t, b_sb):
             nc.scalar.activation(out=pv[t][:].indirect(l5[:]), in_=b_sb, func=COPY)
 
-        def interleave_pair(dst, t0, in0, in1, op):
+        def interleave(dst, in0, in1, op):
             nc.vector.tensor_tensor(
-                out=dst.rearrange("p (c t) -> p c t", t=PACK)[:, :, t0 : t0 + 2],
-                in0=in0[:, t0 : t0 + 2, :].rearrange("p t c -> p c t"),
-                in1=in1[:, t0 : t0 + 2, :].rearrange("p t c -> p c t"),
+                out=dst.rearrange("p (c i t) -> p c t i", i=4, t=PACK),
+                in0=in0.rearrange("p t (c i) -> p c t i", i=4),
+                in1=in1.rearrange("p t (c i) -> p c t i", i=4),
                 op=op,
             )
 
-        b0_ps = psum.tile([P, J], F32, name="b0_ps")
-        b0_sb = tile("b0_sb", [P, J], F32)
-        product_b(0, b0_ps[:])
-        nc.vector.tensor_copy(out=b0_sb[:], in_=b0_ps[:])
-        nc.vector.tensor_copy(out=pv[0][:].indirect(l5[:]), in_=b0_sb[:])
-        b1_ps = psum.tile([P, J], F32, name="b1_ps")
-        b1_sb = tile("b1_sb", [P, J], F32, tag="ta3")
-        product_b(1, b1_ps[:])
-        nc.scalar.copy(out=b1_sb[:], in_=b1_ps[:])
-        scatter_b(1, b1_sb[:])
+        b_sb = []
+        for pair in range(2):
+            b_ps = psum.tile([P, 2, J], F32, name=f"b_ps{pair}")
+            b_pair = tile(f"b_sb{pair}", [P, 2, J], F32)
+            for u in range(2):
+                product_b(2 * pair + u, b_ps[:, u, :])
+                b_sb.append(b_pair[:, u, :])
+            nc.vector.tensor_copy(out=b_pair[:], in_=b_ps[:])
+        scatter_b(0, b_sb[0])
+        scatter_b(1, b_sb[1])
 
         xc = tile("xc", [P, J * PACK], BF16)
         xc_codes = tile("xc_codes", [P, J], U32)
         xc_plane = tile("xc_plane", [P, J], U8)
-        interleave_pair(xc[:], 0, coarse[:], fine[:], ADD)
         for j0 in (0, H):
             xc_half = xc[:, j0 * PACK : (j0 + H) * PACK]
-            interleave_pair(xc_half, 2, coarse[:, :, j0 : j0 + H], fine[:, :, j0 : j0 + H], ADD)
+            interleave(xc_half, coarse[:, :, j0 : j0 + H], fine[:, :, j0 : j0 + H], ADD)
             nc.vector.quantize_mx(out=xc_codes[:, j0 : j0 + H].bitcast(FP8X4), scales=xc_plane[:, j0 : j0 + H], in_=xc_half)
-        for boards, name, tag in ((pw, "pw2", "xo_sb"), (pv, "pv3", "w_plane"), (pw, "pw3", "w_plane_dealt")):
-            boards.append(tile(name, [P, C], F32, tag=tag))
-            nc.gpsimd.memset(boards[-1][:], 0.0)
 
         def product_a(t, j0, j1, out_ps):
             nc.tensor.matmul_mx(
@@ -190,24 +184,19 @@ def tile_picked_refined_plain_two_twoposts_one_plain_kernel(
                 rhs=xc_codes[:, j0:j1].bitcast(FP8X4), rhs_scale=xc_plane[:, j0:j1], start=True, stop=True,
             )
 
-        a0_sb = tile("a0_sb", [P, J], F32)
-        for j0, copy_out in ((0, nc.vector.tensor_copy), (H, nc.scalar.copy)):
+        a_sb = [tile(f"a_sb{t}", [P, J], F32) for t in range(PACK)]
+        for j0 in (0, H):
             a0_ps = psum.tile([P, H], F32, name=f"a0_ps{j0}")
             product_a(0, j0, j0 + H, a0_ps[:])
-            copy_out(out=a0_sb[:, j0 : j0 + H], in_=a0_ps[:])
-        a1_ps = psum.tile([P, J], F32, name="a1_ps")
-        a1_sb = tile("a1_sb", [P, J], F32)
-        product_a(1, 0, J, a1_ps[:])
-        nc.scalar.copy(out=a1_sb[:], in_=a1_ps[:])
-        a_sb = [a0_sb[:], a1_sb[:]]
-        for t in range(2, PACK):
-            ab_ps = psum.tile([P, 2, J], F32, name=f"ab_ps{t}")
-            ab_sb = tile(f"ab_sb{t}", [P, 2, J], F32)
-            product_b(t, ab_ps[:, 1, :])
-            product_a(t, 0, J, ab_ps[:, 0, :])
-            nc.scalar.copy(out=ab_sb[:], in_=ab_ps[:])
-            scatter_b(t, ab_sb[:, 1, :])
-            a_sb.append(ab_sb[:, 0, :])
+            nc.vector.tensor_copy(out=a_sb[0][:, j0 : j0 + H], in_=a0_ps[:])
+        for t in range(1, PACK):
+            a_ps = psum.tile([P, J], F32, name=f"a_ps{t}")
+            product_a(t, 0, J, a_ps[:])
+            nc.scalar.copy(out=a_sb[t][:], in_=a_ps[:])
+        for t, tag in ((2, "w_dealt"), (3, "xc_codes")):
+            pv.append(tile(f"pv{t}", [P, C], F32, tag=tag))
+            nc.gpsimd.memset(pv[t][:], 0.0)
+            scatter_b(t, b_sb[t])
 
         pg = [tile(f"pg{t}", [P, C], F32) for t in range(PACK)]
         first = tile("first", [P, PACK, O], F32)
@@ -223,12 +212,11 @@ def tile_picked_refined_plain_two_twoposts_one_plain_kernel(
             nc.scalar.activation(out=second[:, t, :], in_=pg[t][:].indirect(l7[:]), func=COPY, scale=sb_sb[:, t : t + 1])
 
         hid = tile("hid", [P, O * PACK], BF16)
-        for t0 in (0, 2):
-            interleave_pair(hid[:], t0, first[:], second[:], MAX)
+        interleave(hid[:], first[:], second[:], MAX)
         hid_codes = tile("hid_codes", [P, O], U32)
         hid_plane = tile("hid_plane", [P, O], U8)
         nc.vector.quantize_mx(out=hid_codes[:].bitcast(FP8X4), scales=hid_plane[:], in_=hid[:])
-        for m, (bank, copy_out, queue) in enumerate((("b0_ps", nc.scalar.copy, nc.scalar), ("b1_ps", nc.vector.tensor_copy, nc.sync))):
+        for m, (bank, copy_out, queue) in enumerate((("b_ps0", nc.scalar.copy, nc.scalar), ("b_ps1", nc.vector.tensor_copy, nc.sync))):
             y_ps = psum.tile([P, O], F32, name=f"y_ps{m}", tag=bank)
             y_sb = tile(f"y_sb{m}", [P, O], F32)
             nc.tensor.matmul_mx(

from contextlib import ExitStack

import concourse.mybir as mybir

K, J, R, T, Z, M, C, O, N = 512, 256, 512, 512, 512, 1024, 512, 128, 256
FLOPS = 2 * K * R * J + 2 * Z * R * J + 2 * R * N * O

F32 = mybir.dt.float32
BF16 = mybir.dt.bfloat16
I32 = mybir.dt.int32
U32 = mybir.dt.uint32
U16 = mybir.dt.uint16
U8 = mybir.dt.uint8
FP8X4 = mybir.dt.float8_e4m3fn_x4
FP4X4 = mybir.dt.float4_e2m1fn_x4
COPY = mybir.ActivationFunctionType.Copy
ADD = mybir.AluOpType.add
MAX = mybir.AluOpType.max

P = 128
PACK = 4


def tile_picked_refined_plain_two_twoposts_one_plain_kernel(
    tc, ta, ga, gb, w_words, w_scales, xo_words, xo_scales, w2_words, w2_scales, sa, sb, wb_words, wb_scales,
    offs, offs2, offs3, offs4, offs5, offs6, offs7, out,
):
    nc = tc.nc
    with ExitStack() as ctx:
        keep = ctx.enter_context(tc.tile_pool(name="keep", bufs=1))
        psum = ctx.enter_context(tc.psum_pool(name="psum", bufs=1))

        def tile(name, shape, dtype, tag=None):
            return keep.tile(shape, dtype, name=name, tag=tag or name, align_bytes=64)

        def load_list(name, src):
            dst = keep.tile(list(src.shape), U16, name=name)
            nc.sync.dma_start(dst[:], src)
            return dst

        def load_rowwise(name, src, queue=nc.sync):
            dst = tile(name, [P, PACK], F32)
            queue.dma_start(dst[:], src.rearrange("(p t) one -> p (t one)", t=PACK))
            return dst

        def load_ta(t):
            dst = tile(f"ta{t}", [P, T], F32)
            nc.sync.dma_start(dst[:], ta.rearrange("(p t) c -> p t c", t=PACK)[:, t, :])
            return dst

        def load_bytes(name, src, cols, dtype):
            dst = tile(name, [P, cols], dtype)
            nc.sync.dma_start(dst[:].bitcast(I32), src.bitcast(I32))
            return dst

        def zeroed_plane(name, cols):
            plane = tile(name, [P, cols], U8)
            nc.vector.memset(plane[:].bitcast(I32), 0)
            return plane

        def load_plane(plane, src):
            for q in range(4):
                nc.sync.dma_start(plane[32 * q : 32 * q + 4, :].bitcast(I32), src[0, 4 * q : 4 * q + 4, :].bitcast(I32))

        def load_staged(stage, src):
            nc.sync.dma_start(stage, src[0].bitcast(I32).rearrange("(q r) n -> r q n", r=4))

        def spread(plane, stage):
            for q in range(4):
                nc.vector.tensor_copy(out=plane[32 * q : 32 * q + 4, :].bitcast(I32), in_=stage[:, q, :])

        warm_in = tile("warm_in", [P, 1], F32)
        warm_out = tile("warm_out", [P, 1], F32)
        nc.gpsimd.memset(warm_in[:], 0.0)
        nc.scalar.activation(out=warm_out[:], in_=warm_in[:], func=COPY)

        xo_plane = zeroed_plane("xo_plane", M)
        w2_plane = zeroed_plane("w2_plane", R)
        w_plane = zeroed_plane("w_plane", R)
        wb_plane = zeroed_plane("wb_plane", N)
        pv = [tile(f"pv{t}", [P, C], F32) for t in range(2)]
        pw = [tile(f"pw{t}", [P, C], F32) for t in range(PACK)]
        for board in pv + pw:
            nc.vector.memset(board[:], 0.0)

        xo_stage = tile("xo_stage", [4, 4, M // 4], I32)
        ta_sb = [load_ta(0)]
        l1 = load_list("l1", offs)
        ga_sb = load_rowwise("ga_sb", ga)
        load_staged(xo_stage[:], xo_scales)
        ta_sb.append(load_ta(1))
        xo_sb = load_bytes("xo_sb", xo_words[0], M, U16)
        l3 = load_list("l3", offs3)
        l2 = load_list("l2", offs2)
        gb_sb = load_rowwise("gb_sb", gb)
        ta_sb.append(load_ta(2))
        w2_sb = load_bytes("w2_sb", w2_words[0].rearrange("p n t -> p (n t)"), R, U32)
        load_plane(w2_plane, w2_scales)
        ta_sb.append(load_ta(3))
        w_sb = load_bytes("w_sb", w_words[0], 2 * R, U8)
        l5 = load_list("l5", offs5)
        load_plane(w_plane, w_scales)
        l4 = load_list("l4", offs4)
        l6 = load_list("l6", offs6)
        l7 = load_list("l7", offs7)
        sa_sb = load_rowwise("sa_sb", sa)
        sb_sb = load_rowwise("sb_sb", sb)
        wb_sb = load_bytes("wb_sb", wb_words[0].rearrange("p n t -> p (n t)"), N, U32)
        load_plane(wb_plane, wb_scales)

        H = J // 2
        coarse = tile("coarse", [P, PACK, J], F32)
        fine = tile("fine", [P, PACK, J], F32)

        def fetch_codes(t, j0, j1):
            cols = slice(j0 // 16, j1 // 16)
            nc.scalar.activation(out=coarse[:, t, j0:j1], in_=ta_sb[t][:].indirect(l1[:, cols]), func=COPY, scale=ga_sb[:, t : t + 1])
            nc.scalar.activation(out=fine[:, t, j0:j1], in_=ta_sb[t][:].indirect(l2[:, cols]), func=COPY, scale=gb_sb[:, t : t + 1])

        for t in range(PACK - 1):
            fetch_codes(t, 0, J)
        fetch_codes(PACK - 1, 0, H)
        fetch_codes(PACK - 1, H, J)

        spread(xo_plane, xo_stage)
        w2_plane_dealt = tile("w2_plane_dealt", [P, PACK, P], U8)
        nc.vector.tensor_copy(out=w2_plane_dealt[:], in_=w2_plane[:].rearrange("p (m t) -> p t m", t=PACK))
        xog = tile("xog", [P, J], U16)
        xog_plane = tile("xog_plane", [P, J], U8)
        nc.vector.tensor_copy(out=xog[:], in_=xo_sb[:].indirect(l3[:]))
        nc.vector.tensor_copy(out=xog_plane[:], in_=xo_plane[:].indirect(l3[:]))
        w2_dealt = tile("w2_dealt", [P, PACK, P], U32)
        nc.vector.tensor_copy(
            out=w2_dealt[:].rearrange("p t (c i) -> p c t i", i=4),
            in_=w2_sb[:].rearrange("p (c i t) -> p c t i", i=4, t=PACK),
        )
        w_dealt = tile("w_dealt", [P, PACK, 2 * P], U8)
        w_plane_dealt = tile("w_plane_dealt", [P, PACK, P], U8)
        nc.gpsimd.tensor_copy(
            out=w_dealt[:].rearrange("p t (m two) -> p t m two", two=2),
            in_=w_sb[:].rearrange("p (m t two) -> p t m two", t=PACK, two=2),
        )
        nc.gpsimd.tensor_copy(out=w_plane_dealt[:], in_=w_plane[:].rearrange("p (m t) -> p t m", t=PACK))

        def product_b(t, out_ps):
            nc.tensor.matmul_mx(
                out=out_ps, lhsT=w2_dealt[:, t, :].bitcast(FP8X4), lhsT_scale=w2_plane_dealt[:, t, :],
                rhs=xog[:].bitcast(FP4X4), rhs_scale=xog_plane[:], start=True, stop=True,
            )

        def scatter_b(t, b_sb):
            nc.scalar.activation(out=pv[t][:].indirect(l5[:]), in_=b_sb, func=COPY)

        def interleave(dst, in0, in1, op):
            nc.vector.tensor_tensor(
                out=dst.rearrange("p (c i t) -> p c t i", i=4, t=PACK),
                in0=in0.rearrange("p t (c i) -> p c t i", i=4),
                in1=in1.rearrange("p t (c i) -> p c t i", i=4),
                op=op,
            )

        b_sb = []
        for pair in range(2):
            b_ps = psum.tile([P, 2, J], F32, name=f"b_ps{pair}")
            b_pair = tile(f"b_sb{pair}", [P, 2, J], F32)
            for u in range(2):
                product_b(2 * pair + u, b_ps[:, u, :])
                b_sb.append(b_pair[:, u, :])
            nc.vector.tensor_copy(out=b_pair[:], in_=b_ps[:])
        scatter_b(0, b_sb[0])
        scatter_b(1, b_sb[1])

        xc = tile("xc", [P, J * PACK], BF16)
        xc_codes = tile("xc_codes", [P, J], U32)
        xc_plane = tile("xc_plane", [P, J], U8)
        for j0 in (0, H):
            xc_half = xc[:, j0 * PACK : (j0 + H) * PACK]
            interleave(xc_half, coarse[:, :, j0 : j0 + H], fine[:, :, j0 : j0 + H], ADD)
            nc.vector.quantize_mx(out=xc_codes[:, j0 : j0 + H].bitcast(FP8X4), scales=xc_plane[:, j0 : j0 + H], in_=xc_half)

        def product_a(t, j0, j1, out_ps):
            nc.tensor.matmul_mx(
                out=out_ps, lhsT=w_dealt[:, t, :].bitcast(FP4X4), lhsT_scale=w_plane_dealt[:, t, :],
                rhs=xc_codes[:, j0:j1].bitcast(FP8X4), rhs_scale=xc_plane[:, j0:j1], start=True, stop=True,
            )

        a_sb = [tile(f"a_sb{t}", [P, J], F32) for t in range(PACK)]
        for j0 in (0, H):
            a0_ps = psum.tile([P, H], F32, name=f"a0_ps{j0}")
            product_a(0, j0, j0 + H, a0_ps[:])
            nc.vector.tensor_copy(out=a_sb[0][:, j0 : j0 + H], in_=a0_ps[:])
        for t in range(1, PACK):
            a_ps = psum.tile([P, J], F32, name=f"a_ps{t}")
            product_a(t, 0, J, a_ps[:])
            nc.scalar.copy(out=a_sb[t][:], in_=a_ps[:])
        for t, tag in ((2, "w_dealt"), (3, "xc_codes")):
            pv.append(tile(f"pv{t}", [P, C], F32, tag=tag))
            nc.gpsimd.memset(pv[t][:], 0.0)
            scatter_b(t, b_sb[t])

        pg = [tile(f"pg{t}", [P, C], F32) for t in range(PACK)]
        first = tile("first", [P, PACK, O], F32)
        second = tile("second", [P, PACK, O], F32)
        for t in range(PACK):
            for j0, j1 in ((0, H), (H, J)) if t == 0 else ((0, J),):
                nc.vector.tensor_copy(out=pw[t][:].indirect(l4[:, j0 // 16 : j1 // 16]), in_=a_sb[t][:, j0:j1])
            split = 8 if t == PACK - 1 else C
            nc.gpsimd.tensor_tensor(out=pg[t][:, :split], in0=pw[t][:, :split], in1=pv[t][:, :split], op=ADD)
            if split < C:
                nc.vector.tensor_tensor(out=pg[t][:, split:], in0=pw[t][:, split:], in1=pv[t][:, split:], op=ADD)
            nc.scalar.activation(out=first[:, t, :], in_=pg[t][:].indirect(l6[:]), func=COPY, scale=sa_sb[:, t : t + 1])
            nc.scalar.activation(out=second[:, t, :], in_=pg[t][:].indirect(l7[:]), func=COPY, scale=sb_sb[:, t : t + 1])

        hid = tile("hid", [P, O * PACK], BF16)
        interleave(hid[:], first[:], second[:], MAX)
        hid_codes = tile("hid_codes", [P, O], U32)
        hid_plane = tile("hid_plane", [P, O], U8)
        nc.vector.quantize_mx(out=hid_codes[:].bitcast(FP8X4), scales=hid_plane[:], in_=hid[:])
        for m, (bank, copy_out, queue) in enumerate((("b_ps0", nc.scalar.copy, nc.scalar), ("b_ps1", nc.vector.tensor_copy, nc.sync))):
            y_ps = psum.tile([P, O], F32, name=f"y_ps{m}", tag=bank)
            y_sb = tile(f"y_sb{m}", [P, O], F32)
            nc.tensor.matmul_mx(
                out=y_ps[:], lhsT=wb_sb[:, m * P : (m + 1) * P].bitcast(FP8X4), lhsT_scale=wb_plane[:, m * P : (m + 1) * P],
                rhs=hid_codes[:].bitcast(FP8X4), rhs_scale=hid_plane[:], start=True, stop=True,
            )
            copy_out(out=y_sb[:], in_=y_ps[:])
            queue.dma_start(out[m * P : (m + 1) * P, :], y_sb[:])
